import numpy as np
import ml_dtypes

BF16 = ml_dtypes.bfloat16


def bf(x):
    return np.asarray(x, np.float32).astype(BF16)


def f32(x):
    return np.asarray(x, np.float32)


def f64(x):
    return np.asarray(x).astype(np.float64)


def striped(idx):
    return np.tile(idx.reshape(-1, 16).T, (8, 1))


S, K, M, N = 256, 128, 128, 192


def setup_inputs():
    return {"base": bf(np.random.standard_normal((M, S))), "x": bf(np.random.standard_normal((K, N))), "w": bf(np.random.standard_normal((K, M)) / np.sqrt(K)), "b": f32(0.5 * np.random.standard_normal((M, 1))), "offs": striped(np.random.permutation(S)[:N])}


def reference(base, x, w, b, offs):
    idx = offs[:16].T.reshape(-1)
    z = f64(base).copy()
    z[:, idx] = f64(w).T @ f64(x)
    return np.maximum(z + f64(b), 0.0)

@@ -1,0 +1,41 @@
+import concourse.mybir as mybir
+from concourse.masks import make_identity
+
+P = 128
+S = 256
+N = 192
+
+FLOPS = 2 * P * P * N
+
+BF16, F32, U16 = mybir.dt.bfloat16, mybir.dt.float32, mybir.dt.uint16
+ADD, MAX = mybir.AluOpType.add, mybir.AluOpType.max
+
+
+def tile_scatter_matmul_kernel(tc, base, x, w, b, offs, out):
+    nc = tc.nc
+    with (
+        tc.tile_pool(name="held", bufs=1) as held,
+        tc.psum_pool(name="psum", bufs=1) as psum,
+    ):
+        offsets = held.tile([P, N // 16], U16, name="offsets")
+        nc.sync.dma_start(offsets[:], offs)
+        base_tile = held.tile([P, S], BF16, name="base_tile")
+        nc.scalar.dma_start(base_tile[:], base)
+        weights = held.tile([P, P], BF16, name="weights")
+        nc.sync.dma_start(weights[:], w)
+        moving = held.tile([P, N], BF16, name="moving")
+        nc.sync.dma_start(moving[:], x)
+        bias = held.tile([P, 1], F32, name="bias")
+        nc.scalar.dma_start(bias[:], b)
+
+        ident = held.tile([P, P], BF16, name="ident")
+        make_identity(nc, ident[:])
+
+        window = psum.tile([P, S], F32, name="window")
+        nc.tensor.matmul(window[:], ident[:], base_tile[:], start=True, stop=True)
+
+        nc.tensor.matmul(window[:].indirect(offsets[:]), weights[:], moving[:], start=True, stop=True)
+
+        result = held.tile([P, S], F32, name="result")
+        nc.vector.tensor_scalar(result[:], window[:], bias[:, 0:1], 0.0, op0=ADD, op1=MAX)
+        nc.sync.dma_start(out, result[:])

@@ -4,6 +4,7 @@ from concourse.masks import make_identity
 P = 128
 S = 256
 N = 192
+HALF = S // 2
 
 FLOPS = 2 * P * P * N
 
@@ -21,12 +22,12 @@ def tile_scatter_matmul_kernel(tc, base, x, w, b, offs, out):
         nc.sync.dma_start(offsets[:], offs)
         base_tile = held.tile([P, S], BF16, name="base_tile")
         nc.scalar.dma_start(base_tile[:], base)
-        weights = held.tile([P, P], BF16, name="weights")
-        nc.sync.dma_start(weights[:], w)
         moving = held.tile([P, N], BF16, name="moving")
         nc.sync.dma_start(moving[:], x)
+        weights = held.tile([P, P], BF16, name="weights")
+        nc.scalar.dma_start(weights[:], w)
         bias = held.tile([P, 1], F32, name="bias")
-        nc.scalar.dma_start(bias[:], b)
+        nc.sync.dma_start(bias[:], b)
 
         ident = held.tile([P, P], BF16, name="ident")
         make_identity(nc, ident[:])
@@ -36,6 +37,9 @@ def tile_scatter_matmul_kernel(tc, base, x, w, b, offs, out):
 
         nc.tensor.matmul(window[:].indirect(offsets[:]), weights[:], moving[:], start=True, stop=True)
 
-        result = held.tile([P, S], F32, name="result")
-        nc.vector.tensor_scalar(result[:], window[:], bias[:, 0:1], 0.0, op0=ADD, op1=MAX)
-        nc.sync.dma_start(out, result[:])
+        left = held.tile([P, HALF], F32, name="left")
+        nc.vector.tensor_scalar(left[:], window[:, 0:HALF], bias[:, 0:1], 0.0, op0=ADD, op1=MAX)
+        nc.sync.dma_start(out[:, 0:HALF], left[:])
+        right = held.tile([P, HALF], F32, name="right")
+        nc.vector.tensor_scalar(right[:], window[:, HALF:S], bias[:, 0:1], 0.0, op0=ADD, op1=MAX)
+        nc.scalar.dma_start(out[:, HALF:S], right[:])

@@ -4,7 +4,6 @@ from concourse.masks import make_identity
 P = 128
 S = 256
 N = 192
-HALF = S // 2
 
 FLOPS = 2 * P * P * N
 
@@ -37,9 +36,6 @@ def tile_scatter_matmul_kernel(tc, base, x, w, b, offs, out):
 
         nc.tensor.matmul(window[:].indirect(offsets[:]), weights[:], moving[:], start=True, stop=True)
 
-        left = held.tile([P, HALF], F32, name="left")
-        nc.vector.tensor_scalar(left[:], window[:, 0:HALF], bias[:, 0:1], 0.0, op0=ADD, op1=MAX)
-        nc.sync.dma_start(out[:, 0:HALF], left[:])
-        right = held.tile([P, HALF], F32, name="right")
-        nc.vector.tensor_scalar(right[:], window[:, HALF:S], bias[:, 0:1], 0.0, op0=ADD, op1=MAX)
-        nc.scalar.dma_start(out[:, HALF:S], right[:])
+        result = held.tile([P, S], F32, name="result")
+        nc.vector.tensor_scalar(result[:], window[:], bias[:, 0:1], 0.0, op0=ADD, op1=MAX)
+        nc.scalar.dma_start(out, result[:])

@@ -26,7 +26,7 @@ def tile_scatter_matmul_kernel(tc, base, x, w, b, offs, out):
         weights = held.tile([P, P], BF16, name="weights")
         nc.scalar.dma_start(weights[:], w)
         bias = held.tile([P, 1], F32, name="bias")
-        nc.sync.dma_start(bias[:], b)
+        nc.scalar.dma_start(bias[:], b)
 
         ident = held.tile([P, P], BF16, name="ident")
         make_identity(nc, ident[:])
@@ -38,4 +38,4 @@ def tile_scatter_matmul_kernel(tc, base, x, w, b, offs, out):
 
         result = held.tile([P, S], F32, name="result")
         nc.vector.tensor_scalar(result[:], window[:], bias[:, 0:1], 0.0, op0=ADD, op1=MAX)
-        nc.scalar.dma_start(out, result[:])
+        nc.sync.dma_start(out, result[:])

@@ -4,6 +4,8 @@ from concourse.masks import make_identity
 P = 128
 S = 256
 N = 192
+BANK = 512
+WARM_WIDTHS = (BANK, BANK, BANK // 2)
 
 FLOPS = 2 * P * P * N
 
@@ -30,6 +32,12 @@ def tile_scatter_matmul_kernel(tc, base, x, w, b, offs, out):
 
         ident = held.tile([P, P], BF16, name="ident")
         make_identity(nc, ident[:])
+
+        zeros = held.tile([P, BANK], BF16, name="zeros")
+        nc.vector.memset(zeros[:], 0.0)
+        spare = psum.tile([P, BANK], F32, name="spare")
+        for width in WARM_WIDTHS:
+            nc.tensor.matmul(spare[:, 0:width], zeros[:, 0:P], zeros[:, 0:width], start=True, stop=True)
 
         window = psum.tile([P, S], F32, name="window")
         nc.tensor.matmul(window[:], ident[:], base_tile[:], start=True, stop=True)

@@ -4,8 +4,7 @@ from concourse.masks import make_identity
 P = 128
 S = 256
 N = 192
-BANK = 512
-WARM_WIDTHS = (BANK, BANK, BANK // 2)
+WARM_MATMULS = 10
 
 FLOPS = 2 * P * P * N
 
@@ -33,11 +32,11 @@ def tile_scatter_matmul_kernel(tc, base, x, w, b, offs, out):
         ident = held.tile([P, P], BF16, name="ident")
         make_identity(nc, ident[:])
 
-        zeros = held.tile([P, BANK], BF16, name="zeros")
+        zeros = held.tile([P, P], BF16, name="zeros")
         nc.vector.memset(zeros[:], 0.0)
-        spare = psum.tile([P, BANK], F32, name="spare")
-        for width in WARM_WIDTHS:
-            nc.tensor.matmul(spare[:, 0:width], zeros[:, 0:P], zeros[:, 0:width], start=True, stop=True)
+        spare = psum.tile([P, P], F32, name="spare")
+        for step in range(WARM_MATMULS):
+            nc.tensor.matmul(spare[:], zeros[:], zeros[:], start=True, stop=True)
 
         window = psum.tile([P, S], F32, name="window")
         nc.tensor.matmul(window[:], ident[:], base_tile[:], start=True, stop=True)

@@ -3,6 +3,7 @@ from concourse.masks import make_identity
 
 P = 128
 S = 256
+HALF = S // 2
 N = 192
 WARM_MATMULS = 10
 
@@ -43,6 +44,8 @@ def tile_scatter_matmul_kernel(tc, base, x, w, b, offs, out):
 
         nc.tensor.matmul(window[:].indirect(offsets[:]), weights[:], moving[:], start=True, stop=True)
 
-        result = held.tile([P, S], F32, name="result")
-        nc.vector.tensor_scalar(result[:], window[:], bias[:, 0:1], 0.0, op0=ADD, op1=MAX)
-        nc.sync.dma_start(out, result[:])
+        for half in range(2):
+            columns = slice(half * HALF, (half + 1) * HALF)
+            result = held.tile([P, HALF], F32, name=f"result{half}")
+            nc.vector.tensor_scalar(result[:], window[:, columns], bias[:, 0:1], 0.0, op0=ADD, op1=MAX)
+            nc.sync.dma_start(out[:, columns], result[:])

@@ -19,14 +19,14 @@ def tile_scatter_matmul_kernel(tc, base, x, w, b, offs, out):
         tc.tile_pool(name="held", bufs=1) as held,
         tc.psum_pool(name="psum", bufs=1) as psum,
     ):
-        offsets = held.tile([P, N // 16], U16, name="offsets")
-        nc.sync.dma_start(offsets[:], offs)
         base_tile = held.tile([P, S], BF16, name="base_tile")
-        nc.scalar.dma_start(base_tile[:], base)
-        moving = held.tile([P, N], BF16, name="moving")
-        nc.sync.dma_start(moving[:], x)
+        nc.sync.dma_start(base_tile[:], base)
         weights = held.tile([P, P], BF16, name="weights")
         nc.scalar.dma_start(weights[:], w)
+        offsets = held.tile([P, N // 16], U16, name="offsets")
+        nc.sync.dma_start(offsets[:], offs)
+        moving = held.tile([P, N], BF16, name="moving")
+        nc.scalar.dma_start(moving[:], x)
         bias = held.tile([P, 1], F32, name="bias")
         nc.scalar.dma_start(bias[:], b)
 

@@ -28,7 +28,7 @@ def tile_scatter_matmul_kernel(tc, base, x, w, b, offs, out):
         moving = held.tile([P, N], BF16, name="moving")
         nc.scalar.dma_start(moving[:], x)
         bias = held.tile([P, 1], F32, name="bias")
-        nc.scalar.dma_start(bias[:], b)
+        nc.sync.dma_start(bias[:], b)
 
         ident = held.tile([P, P], BF16, name="ident")
         make_identity(nc, ident[:])
@@ -48,4 +48,4 @@ def tile_scatter_matmul_kernel(tc, base, x, w, b, offs, out):
             columns = slice(half * HALF, (half + 1) * HALF)
             result = held.tile([P, HALF], F32, name=f"result{half}")
             nc.vector.tensor_scalar(result[:], window[:, columns], bias[:, 0:1], 0.0, op0=ADD, op1=MAX)
-            nc.sync.dma_start(out[:, columns], result[:])
+            nc.scalar.dma_start(out[:, columns], result[:])

import concourse.mybir as mybir
from concourse.masks import make_identity

P = 128
S = 256
HALF = S // 2
N = 192
WARM_MATMULS = 10

FLOPS = 2 * P * P * N

BF16, F32, U16 = mybir.dt.bfloat16, mybir.dt.float32, mybir.dt.uint16
ADD, MAX = mybir.AluOpType.add, mybir.AluOpType.max


def tile_scatter_matmul_kernel(tc, base, x, w, b, offs, out):
    nc = tc.nc
    with (
        tc.tile_pool(name="held", bufs=1) as held,
        tc.psum_pool(name="psum", bufs=1) as psum,
    ):
        base_tile = held.tile([P, S], BF16, name="base_tile")
        nc.sync.dma_start(base_tile[:], base)
        weights = held.tile([P, P], BF16, name="weights")
        nc.scalar.dma_start(weights[:], w)
        offsets = held.tile([P, N // 16], U16, name="offsets")
        nc.sync.dma_start(offsets[:], offs)
        moving = held.tile([P, N], BF16, name="moving")
        nc.scalar.dma_start(moving[:], x)
        bias = held.tile([P, 1], F32, name="bias")
        nc.sync.dma_start(bias[:], b)

        ident = held.tile([P, P], BF16, name="ident")
        make_identity(nc, ident[:])

        zeros = held.tile([P, P], BF16, name="zeros")
        nc.vector.memset(zeros[:], 0.0)
        spare = psum.tile([P, P], F32, name="spare")
        for step in range(WARM_MATMULS):
            nc.tensor.matmul(spare[:], zeros[:], zeros[:], start=True, stop=True)

        window = psum.tile([P, S], F32, name="window")
        nc.tensor.matmul(window[:], ident[:], base_tile[:], start=True, stop=True)

        nc.tensor.matmul(window[:].indirect(offsets[:]), weights[:], moving[:], start=True, stop=True)

        for half in range(2):
            columns = slice(half * HALF, (half + 1) * HALF)
            result = held.tile([P, HALF], F32, name=f"result{half}")
            nc.vector.tensor_scalar(result[:], window[:, columns], bias[:, 0:1], 0.0, op0=ADD, op1=MAX)
            nc.scalar.dma_start(out[:, columns], result[:])
